import numpy as np, ml_dtypes
CORES = [2,10,34,50,74,82,98,114,130,138,162,178,202,210,226,242]
N = 16
F, TK = 64, 64
def setup_inputs(rng):
    return {"x": rng.standard_normal((N, 128, N * TK), dtype=np.float32).astype(ml_dtypes.bfloat16), "w": rng.standard_normal((N, 128, F), dtype=np.float32).astype(ml_dtypes.bfloat16)}
def setup_inputs_big(rng):
    d = setup_inputs(rng)
    for k in ("x", "w"): d[k] = (d[k].astype(np.float32) * 1024.0).astype(d[k].dtype)
    return d
def setup_inputs_small(rng):
    d = setup_inputs(rng)
    for k in ("x", "w"): d[k] = (d[k].astype(np.float32) * (1 / 1024.0)).astype(d[k].dtype)
    return d
def reference(x, w):
    X, W = x.astype(np.float64), w.astype(np.float64)
    y = np.zeros((N, F, N * TK))
    for r in range(N):
        for j in range(N):
            y[r][:, TK * j:TK * j + TK] = W[r].T @ X[j][:, TK * r:TK * r + TK]
    return {"y": y.astype(ml_dtypes.bfloat16 if x.dtype != np.float64 else np.float64)}

from concourse.bass import DstId, RemoteDMATransfer

N, TK, F = 16, 64, 64

LOADS = [("sync", 8, 8), ("scalar", 0, 8)]
RANK_CALLS = [
    [("send", 8, 8, 1)],
    [("send", 4, 4, 2)],
    [("send", 2, 2, 4)],
    [("send", 1, 1, 8)],
]
HELPER_CALLS = []
GROUPS = [(0, 1), (8, 8), (4, 4), (2, 2), (1, 1)]
STORES = [("sync", 8, 8), ("scalar", 4, 4), ("sync", 2, 2), ("scalar", 0, 2)]

SCRATCH = {
    "xs": ("sbuf", [128, N * TK], "bfloat16"),
    "ws": ("sbuf", [128, F], "bfloat16"),
    "land": ("sbuf", [128, N * TK], "bfloat16"),
    "ysb": ("sbuf", [F, N * TK], "bfloat16"),
}
SEMAPHORES = ["ldw", "sent", "hin", "stored"]
for _q, _m0, _s in LOADS:
    SEMAPHORES.append("ld%d" % _m0)
for _m0, _s in GROUPS:
    SCRATCH["ps%d" % _m0] = ("psum", [128, 512], "float32")
    SEMAPHORES += ["arr%d" % _m0, "mm%d" % _m0, "cp%d" % _m0]


def _cols(j, m0, s):
    a = ((j ^ m0) // s) * s
    return a * TK, (a + s) * TK


def _inside(m, run):
    return run[0] <= m < run[0] + run[1]


def _group_of(m):
    return [gr for gr in GROUPS if _inside(m, gr)][0]


def _engines_per_block():
    out = {}
    for calls in [RANK_CALLS] + HELPER_CALLS:
        for call in calls:
            for it in call:
                if it[0] == "send":
                    for m in range(it[1], it[1] + it[2]):
                        out[m] = it[3]
    return out


def _same_chip(topo, a, b):
    return topo.host(a) == topo.host(b) and topo.chip(a) == topo.chip(b)


def _helpers(topo, T, owner, sim_cores):
    cand = [c for c in range(sim_cores) if c != owner and _same_chip(topo, c, owner)
            and all(topo.may_write(c, d) for d in T.cores if d != owner)]
    cand.sort(key=lambda c: (topo.die(c) == topo.die(owner), c))
    return cand


def _issue(g, core, j, call, T, topo, helpers):
    todo = []
    for it in call:
        if it[0] == "send":
            for m in range(it[1], it[1] + it[2]):
                r = j ^ m
                todo.append((T.cores[r], T.xs[:, r * TK:(r + 1) * TK], T.land[:, j * TK:(j + 1) * TK],
                             T.sem["arr%d" % _group_of(m)[0]], it[3]))
        else:
            a, b = _cols(j, it[1], it[2])
            todo.append((helpers[it[4]], T.xs[:, a:b], T.xs[:, a:b], T.sem.hin, it[3]))
    common = topo.mask(core, todo[0][0])
    far = common
    for d in T.cores:
        if not _same_chip(topo, d, core):
            far &= topo.mask(core, d)
    for t in todo:
        common &= topo.mask(core, t[0])
    engines = [e for e in range(common.bit_length()) if (common >> e) & 1]
    engines.sort(key=lambda e: (((far >> e) & 1) == 0, e))
    pos, transfers = 0, []
    for dst, src_ap, dst_ap, sem, ne in todo:
        mask = 0
        for e in engines[pos:pos + ne]:
            mask |= 1 << e
        pos += ne
        rid, pid = topo.addr(dst, core)
        transfers.append(RemoteDMATransfer(dst_ids=[DstId(rid=rid, pnc=pid)], dma_engine_mask=mask, remote_sem=sem,
                                           src=src_ap, dst=dst_ap))
    assert pos <= len(engines)
    g.remote_dma_fused(transfers, local_sem=T.sem.sent)
    return pos


def _helper_program(g, core, T, topo, sim_cores):
    owners = [c for c in T.cores if _same_chip(topo, c, core)]
    if not owners or not HELPER_CALLS:
        return
    owner = owners[0]
    helpers = _helpers(topo, T, owner, sim_cores)[:len(HELPER_CALLS)]
    if core not in helpers:
        return
    h = helpers.index(core)
    got = sum(it[3] for call in RANK_CALLS for it in call if it[0] == "give" and it[4] == h)
    g.wait_ge(T.sem.hin, got)
    sent = 0
    for call in HELPER_CALLS[h]:
        sent += _issue(g, core, T.rank_of(owner), call, T, topo, helpers)
    g.wait_ge(T.sem.sent, sent)


def rank_program(g, core, T, topo):
    sim_cores = 256
    rank = T.rank_of(core)
    if rank is None:
        _helper_program(g, core, T, topo, sim_cores)
        return
    queue = {"sync": g.sync, "scalar": g.scalar}
    helpers = _helpers(topo, T, core, sim_cores)

    for qn, m0, s in LOADS:
        a, b = _cols(rank, m0, s)
        queue[qn].dma_start(T.xs[:, a:b], T.x[:, a:b]).then_inc(T.sem["ld%d" % m0], 16)
    g.sync.dma_start(T.ws[:, :], T.w[:, :]).then_inc(T.sem.ldw, 16)

    waited, sent = [], 0
    for call in RANK_CALLS:
        for qn, m0, s in LOADS:
            if m0 not in waited and any(_inside(it[1], (m0, s)) for it in call):
                g.wait_ge(T.sem["ld%d" % m0], 16)
                waited.append(m0)
        sent += _issue(g, core, rank, call, T, topo, helpers)

    per_block = _engines_per_block()
    for m0, s in GROUPS:
        a, b = _cols(rank, m0, s)
        if m0 == 0:
            g.tensor.wait_ge(T.sem.ldw, 16)
            g.tensor.wait_ge(T.sem["ld%d" % [l for l in LOADS if _inside(0, (l[1], l[2]))][0][1]], 16)
            rhs = T.xs[:, a:b]
        else:
            g.tensor.wait_ge(T.sem["arr%d" % m0], sum(per_block[m] for m in range(m0, m0 + s)))
            rhs = T.land[:, a:b]
        ps = T["ps%d" % m0][0:F, 0:b - a]
        g.tensor.matmul(ps, T.ws[:, :], rhs, True, True).then_inc(T.sem["mm%d" % m0], 1)
        g.vector.wait_ge(T.sem["mm%d" % m0], 1)
        g.vector.tensor_copy(T.ysb[:, a:b], ps).then_inc(T.sem["cp%d" % m0], 1)

    for qn, m0, s in STORES:
        a, b = _cols(rank, m0, s)
        for gm, gs in GROUPS:
            if _inside(gm, (m0, s)):
                queue[qn].wait_ge(T.sem["cp%d" % gm], 1)
        queue[qn].dma_start(T.y[:, a:b], T.ysb[:, a:b]).then_inc(T.sem.stored, 16)

    g.wait_ge(T.sem.sent, sent)
    g.wait_ge(T.sem.stored, 16 * len(STORES))
